import numpy as np
import ml_dtypes


def mxq(x, axis, fmt="e4m3"):
    dtype, down = {"e4m3": (ml_dtypes.float8_e4m3fn, 7), "e5m2": (ml_dtypes.float8_e5m2, 14)}[fmt]
    v = np.moveaxis(np.asarray(x, np.float32).astype(ml_dtypes.bfloat16).astype(np.float64), axis, -1)
    blocks = v.reshape(v.shape[:-1] + (-1, 32))
    amax = np.abs(blocks).max(-1, keepdims=True)
    byte = np.maximum(np.where(amax > 0, np.frexp(amax)[1] - 1 + 127, 0) - down, 1)
    scale = np.exp2(byte - 127.0)
    codes = (blocks / scale).astype(np.float32).astype(dtype).astype(np.float64)
    return np.moveaxis((codes * scale).reshape(v.shape), -1, axis)


WIDE = False


def mx_kscale(k):
    if not WIDE:
        return np.ones(k)
    levels = np.array([10, -10, 5, -5, 0])
    if k % 512:
        return np.exp2(np.random.permutation(np.resize(levels, k // 32))).repeat(32)
    a = np.empty((k // 512, 16))
    for p in range(k // 512):
        a[p, :8] = np.random.permutation(np.resize(levels, 8))
        for g in range(8):
            far = levels[np.abs(levels - a[p, g]) >= 10]
            a[p, g + 8] = far[np.random.randint(len(far))]
    return np.exp2(a.ravel()).repeat(32)


def f64(x):
    return np.asarray(x).astype(np.float64)


def striped(idx):
    return np.tile(idx.reshape(-1, 16).T, (8, 1)).astype(np.uint16)


def unstriped(offs):
    return offs[:16].T.reshape(-1).astype(np.int64)


def pack_weight(w):
    k, n = w.shape
    w = f64(np.asarray(w, np.float32).astype(ml_dtypes.bfloat16)).reshape(k // 32, 32, n)
    amax = np.abs(w).max(1)
    byte = np.clip(np.where(amax > 0, np.frexp(amax)[1] - 1 + 127 - 7, 1), 1, 254)
    scaled = (w * np.exp2(127.0 - byte)[:, None, :]).reshape(k, n).astype(np.float32)
    words = np.ascontiguousarray(scaled.reshape(k // 512, 128, 4, n).transpose(0, 1, 3, 2)).astype(ml_dtypes.float8_e4m3fn).view(np.uint8)
    return words, np.ascontiguousarray(byte.astype(np.uint8).reshape(k // 512, 16, n))


def unpack_weight(words, scales):
    g, p, n, _ = words.shape
    vals = np.ascontiguousarray(words).view(ml_dtypes.float8_e4m3fn).astype(np.float64) * np.repeat(np.exp2(scales.astype(np.float64) - 127.0), 8, axis=1)[..., None]
    return vals.transpose(0, 1, 3, 2).reshape(g * 512, n)


K, T, S, N, H, U = 512, 2048, 512, 256, 512, 1024


def setup_inputs():
    n = np.random.standard_normal
    s = mx_kscale(K)[:, None]
    u = mx_kscale(H)
    packed_xT = pack_weight(n((K, T)) * s)
    return {
        "x_words": packed_xT[0],
        "x_scales": packed_xT[1],
        "w1": (n((K, H)) / np.sqrt(K) / s).astype(np.float32),
        "w2": (n((K, H)) / np.sqrt(K) / s).astype(np.float32),
        "unit": (np.random.uniform(0.6, 1.4, (H, 1)) * u[:, None]).astype(np.float32),
        "w3": (n((H, N)) / np.sqrt(H) / u[:, None]).astype(np.float32),
        "offs": striped(np.random.permutation(T)[:S]),
        "fa": striped(np.random.permutation(np.concatenate([np.arange(S), np.random.randint(0, S, U - S)]))),
        "fb": striped(np.random.permutation(np.concatenate([np.arange(S), np.random.randint(0, S, U - S)]))),
    }


def reference(x_words, x_scales, w1, w2, unit, w3, offs, fa, fb):
    xq = unpack_weight(x_words, x_scales)[:, unstriped(offs)]
    y = mxq(f64(w1), 0, "e4m3").T @ xq
    ya = y[:, unstriped(fa)]
    z1 = mxq(f64(w2), 0, "e4m3").T @ xq
    za = z1[:, unstriped(fa)]
    scr = ya + 0.5 * za
    zb_ = z1[:, unstriped(fb)]
    yb_ = y[:, unstriped(fb)]
    hid = f64(unit) * (np.maximum(scr, 0.8 * zb_) - yb_)
    return mxq(f64(w3), 0, "e4m3").T @ mxq(hid, 0, "e4m3")

@@ -1,0 +1,200 @@
+from contextlib import ExitStack
+
+import concourse.mybir as mybir
+
+K, T, S, N, H, U = 512, 2048, 512, 256, 512, 1024
+FLOPS = 2 * (2 * K * H * S + H * N * U)
+
+F32 = mybir.dt.float32
+BF16 = mybir.dt.bfloat16
+I32 = mybir.dt.int32
+U32 = mybir.dt.uint32
+U16 = mybir.dt.uint16
+U8 = mybir.dt.uint8
+FP8X4 = mybir.dt.float8_e4m3fn_x4
+ALU = mybir.AluOpType
+ACT = mybir.ActivationFunctionType
+
+P = 128
+PACK = 4
+HALF = H // 2
+CHUNK = 256
+CHUNKS = U // CHUNK
+WINDOW = S + 32
+SPANS = ((0, 512), (512, 768), (768, 1024))
+STEPS = ((0, 256), (256, 512), (512, 768), (768, 896), (896, 1024))
+SPLIT = 88
+
+
+def tile_picked_yfairsp_cap_p_kernel(
+    tc, x_words, x_scales, w1, w2, unit, w3, offs, fa, fb, out
+):
+    nc = tc.nc
+    with ExitStack() as ctx:
+        keep = ctx.enter_context(tc.tile_pool(name="keep", bufs=1))
+        psum = ctx.enter_context(tc.psum_pool(name="psum", bufs=8))
+
+        offs_sb = keep.tile([P, S // 16], U16, name="offs_sb")
+        fa_sb = keep.tile([P, U // 16], U16, name="fa_sb")
+        fb_sb = keep.tile([P, U // 16], U16, name="fb_sb")
+        words = keep.tile([P, T], I32, name="words", align_bytes=64)
+        scales = keep.tile([P, T], U8, name="scales", align_bytes=64)
+        unit_sb = keep.tile([P, PACK], F32, name="unit_sb")
+        w3_raw = keep.tile([P, PACK, N], F32, name="w3_raw")
+
+        nc.vector.memset(scales[:].bitcast(I32), 0)
+        nc.sync.dma_start(offs_sb[:], offs)
+        nc.sync.dma_start(words[:], x_words[0].rearrange("p c r -> p (c r)").bitcast(I32))
+        for q in range(4):
+            nc.scalar.dma_start(
+                scales[32 * q : 32 * q + 4, :].bitcast(I32), x_scales[0, 4 * q : 4 * q + 4, :].bitcast(I32)
+            )
+        nc.sync.dma_start(unit_sb[:], unit.rearrange("(p t) o -> p (t o)", t=PACK))
+        raw = {}
+        for name, w in (("w1", w1), ("w2", w2)):
+            rows = w.rearrange("(p j) c -> p j c", j=PACK)
+            for h in range(2):
+                raw[name, h] = keep.tile([P, PACK, HALF], F32, name="%s_raw%d" % (name, h))
+                nc.sync.dma_start(raw[name, h][:], rows[:, :, h * HALF : (h + 1) * HALF])
+            if name == "w1":
+                nc.sync.dma_start(fb_sb[:], fb)
+        nc.sync.dma_start(fa_sb[:], fa)
+        nc.sync.dma_start(w3_raw[:], w3.rearrange("(p j) m -> p j m", j=PACK))
+
+        mag = keep.tile([P, PACK], F32, name="mag")
+        neg = keep.tile([P, PACK], F32, name="neg")
+        half = keep.tile([P, PACK], F32, name="half")
+        most = keep.tile([P, PACK], F32, name="most")
+        step = keep.tile([P, PACK], F32, name="step")
+        sgn = keep.tile([P, PACK], F32, name="sgn")
+        nc.scalar.activation(mag[:], unit_sb[:], ACT.Abs)
+        nc.scalar.activation(neg[:], mag[:], ACT.Copy, scale=-1.0)
+        nc.scalar.activation(half[:], mag[:], ACT.Copy, scale=0.5)
+        nc.scalar.activation(most[:], mag[:], ACT.Copy, scale=0.8)
+        nc.vector.tensor_scalar(step[:], unit_sb[:], 0.0, 2.0, ALU.is_ge, ALU.mult)
+        nc.vector.tensor_scalar(sgn[:], step[:], -1.0, None, ALU.add)
+
+        x_codes = keep.tile([P, S], U32, name="x_codes", align_bytes=64)
+        x_plane = keep.tile([P, S], U8, name="x_plane", align_bytes=64)
+        nc.vector.tensor_copy(x_codes[:], words[:].bitcast(U32).indirect(offs_sb[:]))
+        nc.vector.tensor_copy(x_plane[:], scales[:].indirect(offs_sb[:]))
+
+        def deal(name, lo, hi, copy):
+            h = lo // (P // 2)
+            dst = grouped[name][:].rearrange("p t m j -> p m j t")[:, lo:hi, :, :]
+            src = raw[name, h][:].rearrange("p j (m t) -> p m j t", t=PACK)
+            copy(dst, src[:, lo - h * (P // 2) : hi - h * (P // 2), :, :])
+
+        def product(name, t):
+            codes = keep.tile([P, P], U32, name="%s_codes%d" % (name, t), align_bytes=64)
+            plane = keep.tile([P, P], U8, name="%s_plane%d" % (name, t), align_bytes=64)
+            nc.vector.quantize_mx(
+                out=codes[:].bitcast(FP8X4), scales=plane[:], in_=grouped[name][:, t].rearrange("p m j -> p (m j)")
+            )
+            acc = psum.tile([P, S], F32, name="acc")
+            nc.tensor.matmul_mx(
+                out=acc[:], lhsT=codes[:].bitcast(FP8X4), lhsT_scale=plane[:],
+                rhs=x_codes[:].bitcast(FP8X4), rhs_scale=x_plane[:], start=True, stop=True,
+            )
+            return acc
+
+        grouped = {}
+        for name in ("w1", "w2"):
+            grouped[name] = keep.tile([P, PACK, P, PACK], BF16, name="%s_grouped" % name, align_bytes=64)
+        deal("w1", 0, P // 2, nc.scalar.copy)
+        deal("w1", P // 2, SPLIT, nc.scalar.copy)
+        deal("w1", SPLIT, P, nc.vector.tensor_copy)
+        neg_y = []
+        for t in range(PACK):
+            y = product("w1", t)
+            neg_y.append(keep.tile([P, WINDOW], F32, name="neg_y%d" % t))
+            nc.scalar.activation(neg_y[t][:, :S], y[:], ACT.Copy, scale=neg[:, t : t + 1])
+        deal("w2", 0, P // 2, nc.vector.tensor_copy)
+        deal("w2", P // 2, P, nc.vector.tensor_copy)
+        z = [product("w2", t) for t in range(PACK)]
+        score, signal = [], []
+        for t in range(PACK):
+            score.append(keep.tile([P, WINDOW], F32, name="score%d" % t))
+            signal.append(keep.tile([P, WINDOW], F32, name="signal%d" % t))
+            nc.vector.scalar_tensor_tensor(
+                score[t][:, :S], z[t][:], half[:, t : t + 1], neg_y[t][:, :S], ALU.mult, ALU.subtract
+            )
+            nc.vector.scalar_tensor_tensor(
+                signal[t][:, :S], z[t][:], most[:, t : t + 1], neg_y[t][:, :S], ALU.mult, ALU.add
+            )
+
+        w3_grouped = keep.tile([P, N, PACK], BF16, name="w3_grouped", align_bytes=64)
+        w3_codes = keep.tile([P, N], U32, name="w3_codes", align_bytes=64)
+        w3_plane = keep.tile([P, N], U8, name="w3_plane", align_bytes=64)
+        nc.vector.tensor_tensor(
+            w3_grouped[:].rearrange("p (c i) j -> p c j i", i=4),
+            w3_raw[:].rearrange("p j (c i) -> p c j i", i=4),
+            sgn[:].unsqueeze(1).unsqueeze(3).to_broadcast([P, N // 4, PACK, 4]),
+            ALU.mult,
+        )
+        nc.vector.quantize_mx(
+            out=w3_codes[:].bitcast(FP8X4), scales=w3_plane[:], in_=w3_grouped[:].rearrange("p m j -> p (m j)")
+        )
+
+        second_y = {}
+        second_signal = keep.tile([P, PACK, U], F32, name="second_signal")
+        lead = keep.tile([P, PACK, U], F32, name="lead")
+
+        def entries(lst, lo, hi):
+            return lst[:, lo // 16 : hi // 16]
+
+        def fetch_y(lo, hi):
+            for t in range(PACK):
+                second_y[t] = keep.tile([P, hi - lo], F32, name="second_y%d" % t)
+                nc.scalar.activation(second_y[t][:], neg_y[t][:].indirect(entries(fb_sb, lo, hi)), ACT.Copy)
+
+        def fetch_signal(lo, hi):
+            for t in range(PACK):
+                nc.scalar.activation(
+                    second_signal[:, t, lo:hi], signal[t][:].indirect(entries(fb_sb, lo, hi)), ACT.Copy
+                )
+
+        def fetch_score(lo, hi):
+            for t in range(PACK):
+                nc.vector.tensor_tensor(
+                    lead[:, t, lo:hi], score[t][:].indirect(entries(fa_sb, lo, hi)), second_y[t][:], ALU.add
+                )
+
+        def finish(lo, hi):
+            n = hi - lo
+            hid = keep.tile([P, n, PACK], BF16, name="hid%d" % lo, align_bytes=64)
+            codes = keep.tile([P, n], U32, name="hid_codes%d" % lo, align_bytes=64)
+            plane = keep.tile([P, n], U8, name="hid_plane%d" % lo, align_bytes=64)
+            nc.vector.tensor_tensor(
+                hid[:].rearrange("p (c i) t -> p c t i", i=4),
+                lead[:, :, lo:hi].rearrange("p t (c i) -> p c t i", i=4),
+                second_signal[:, :, lo:hi].rearrange("p t (c i) -> p c t i", i=4),
+                ALU.max,
+            )
+            nc.vector.quantize_mx(
+                out=codes[:].bitcast(FP8X4), scales=plane[:], in_=hid[:].rearrange("p r t -> p (r t)")
+            )
+            acc = psum.tile([P, 2, n], F32, name="acc")
+            for mt in range(2):
+                nc.tensor.matmul_mx(
+                    out=acc[:, mt, :],
+                    lhsT=w3_codes[:, mt * P : (mt + 1) * P].bitcast(FP8X4),
+                    lhsT_scale=w3_plane[:, mt * P : (mt + 1) * P],
+                    rhs=codes[:].bitcast(FP8X4), rhs_scale=plane[:], start=True, stop=True,
+                )
+            result = keep.tile([P, 2, n], F32, name="result%d" % lo)
+            nc.scalar.copy(result[:], acc[:])
+            nc.sync.dma_start(out.rearrange("(mt p) r -> p mt r", p=P)[:, :, lo:hi], result[:])
+
+        fetch_y(0, 512)
+        fetch_score(0, 512)
+        fetch_signal(0, 512)
+        fetch_y(512, 1024)
+        finish(0, 256)
+        finish(256, 512)
+        fetch_score(512, 1024)
+        fetch_signal(512, 768)
+        fetch_signal(768, 1024)
+        finish(512, 768)
+        finish(768, 896)
+        finish(896, 1024)

@@ -115,7 +115,7 @@ def tile_picked_yfairsp_cap_p_kernel(
         score, signal = [], []
         for t in range(PACK):
             score.append(keep.tile([P, WINDOW], F32, name="score%d" % t))
-            signal.append(keep.tile([P, WINDOW], F32, name="signal%d" % t))
+            signal.append(keep.tile([P, WINDOW], F32, name="signal%d" % t, tag="signal%d" % t))
             nc.vector.scalar_tensor_tensor(
                 score[t][:, :S], z[t][:], half[:, t : t + 1], neg_y[t][:, :S], ALU.mult, ALU.subtract
             )
@@ -127,9 +127,9 @@ def tile_picked_yfairsp_cap_p_kernel(
         w3_codes = keep.tile([P, N], U32, name="w3_codes", align_bytes=64)
         w3_plane = keep.tile([P, N], U8, name="w3_plane", align_bytes=64)
         nc.vector.tensor_tensor(
-            w3_grouped[:].rearrange("p (c i) j -> p c j i", i=4),
-            w3_raw[:].rearrange("p j (c i) -> p c j i", i=4),
-            sgn[:].unsqueeze(1).unsqueeze(3).to_broadcast([P, N // 4, PACK, 4]),
+            w3_grouped[:].rearrange("p (c i) j -> p c j i", i=2),
+            w3_raw[:].rearrange("p j (c i) -> p c j i", i=2),
+            sgn[:].unsqueeze(1).unsqueeze(3).to_broadcast([P, N // 2, PACK, 2]),
             ALU.mult,
         )
         nc.vector.quantize_mx(
@@ -138,7 +138,7 @@ def tile_picked_yfairsp_cap_p_kernel(
 
         second_y = {}
         second_signal = keep.tile([P, PACK, U], F32, name="second_signal")
-        lead = keep.tile([P, PACK, U], F32, name="lead")
+        lead = {}
 
         def entries(lst, lo, hi):
             return lst[:, lo // 16 : hi // 16]
@@ -155,20 +155,22 @@ def tile_picked_yfairsp_cap_p_kernel(
                 )
 
         def fetch_score(lo, hi):
+            lead[lo] = keep.tile([P, PACK, hi - lo], F32, name="lead")
             for t in range(PACK):
                 nc.vector.tensor_tensor(
-                    lead[:, t, lo:hi], score[t][:].indirect(entries(fa_sb, lo, hi)), second_y[t][:], ALU.add
+                    lead[lo][:, t, :], score[t][:].indirect(entries(fa_sb, lo, hi)), second_y[t][:], ALU.add
                 )
 
         def finish(lo, hi):
             n = hi - lo
+            base = lo // 512 * 512
             hid = keep.tile([P, n, PACK], BF16, name="hid%d" % lo, align_bytes=64)
             codes = keep.tile([P, n], U32, name="hid_codes%d" % lo, align_bytes=64)
             plane = keep.tile([P, n], U8, name="hid_plane%d" % lo, align_bytes=64)
             nc.vector.tensor_tensor(
-                hid[:].rearrange("p (c i) t -> p c t i", i=4),
-                lead[:, :, lo:hi].rearrange("p t (c i) -> p c t i", i=4),
-                second_signal[:, :, lo:hi].rearrange("p t (c i) -> p c t i", i=4),
+                hid[:].rearrange("p (c i) t -> p c t i", i=2),
+                lead[base][:, :, lo - base : hi - base].rearrange("p t (c i) -> p c t i", i=2),
+                second_signal[:, :, lo:hi].rearrange("p t (c i) -> p c t i", i=2),
                 ALU.max,
             )
             nc.vector.quantize_mx(
@@ -182,7 +184,10 @@ def tile_picked_yfairsp_cap_p_kernel(
                     lhsT_scale=w3_plane[:, mt * P : (mt + 1) * P],
                     rhs=codes[:].bitcast(FP8X4), rhs_scale=plane[:], start=True, stop=True,
                 )
-            result = keep.tile([P, 2, n], F32, name="result%d" % lo)
+            return acc
+
+        def store(lo, hi, acc, tag):
+            result = keep.tile([P, 2, hi - lo], F32, name="result%d" % lo, tag=tag)
             nc.scalar.copy(result[:], acc[:])
             nc.sync.dma_start(out.rearrange("(mt p) r -> p mt r", p=P)[:, :, lo:hi], result[:])
 
@@ -190,11 +195,13 @@ def tile_picked_yfairsp_cap_p_kernel(
         fetch_score(0, 512)
         fetch_signal(0, 512)
         fetch_y(512, 1024)
-        finish(0, 256)
-        finish(256, 512)
+        acc0 = finish(0, 256)
+        acc1 = finish(256, 512)
         fetch_score(512, 1024)
         fetch_signal(512, 768)
         fetch_signal(768, 1024)
-        finish(512, 768)
-        finish(768, 896)
-        finish(896, 1024)
+        store(0, 256, acc0, "signal2")
+        store(256, 512, acc1, "signal3")
+        store(512, 768, finish(512, 768), "result2")
+        store(768, 896, finish(768, 896), "result3")
+        store(896, 1024, finish(896, 1024), "result4")

@@ -17,13 +17,8 @@ ACT = mybir.ActivationFunctionType
 
 P = 128
 PACK = 4
-HALF = H // 2
-CHUNK = 256
-CHUNKS = U // CHUNK
 WINDOW = S + 32
-SPANS = ((0, 512), (512, 768), (768, 1024))
-STEPS = ((0, 256), (256, 512), (512, 768), (768, 896), (896, 1024))
-SPLIT = 88
+SPLIT = 44
 
 
 def tile_picked_yfairsp_cap_p_kernel(
@@ -42,23 +37,21 @@ def tile_picked_yfairsp_cap_p_kernel(
         unit_sb = keep.tile([P, PACK], F32, name="unit_sb")
         w3_raw = keep.tile([P, PACK, N], F32, name="w3_raw")
 
-        nc.vector.memset(scales[:].bitcast(I32), 0)
+        nc.vector.memset(scales[:, : T // 2].bitcast(I32), 0)
+        nc.gpsimd.memset(scales[:, T // 2 :].bitcast(I32), 0)
         nc.sync.dma_start(offs_sb[:], offs)
+        nc.sync.dma_start(unit_sb[:], unit.rearrange("(p t) o -> p (t o)", t=PACK))
         nc.sync.dma_start(words[:], x_words[0].rearrange("p c r -> p (c r)").bitcast(I32))
         for q in range(4):
-            nc.scalar.dma_start(
+            nc.sync.dma_start(
                 scales[32 * q : 32 * q + 4, :].bitcast(I32), x_scales[0, 4 * q : 4 * q + 4, :].bitcast(I32)
             )
-        nc.sync.dma_start(unit_sb[:], unit.rearrange("(p t) o -> p (t o)", t=PACK))
+        nc.sync.dma_start(fb_sb[:], fb)
+        nc.sync.dma_start(fa_sb[:], fa)
         raw = {}
         for name, w in (("w1", w1), ("w2", w2)):
-            rows = w.rearrange("(p j) c -> p j c", j=PACK)
-            for h in range(2):
-                raw[name, h] = keep.tile([P, PACK, HALF], F32, name="%s_raw%d" % (name, h))
-                nc.sync.dma_start(raw[name, h][:], rows[:, :, h * HALF : (h + 1) * HALF])
-            if name == "w1":
-                nc.sync.dma_start(fb_sb[:], fb)
-        nc.sync.dma_start(fa_sb[:], fa)
+            raw[name] = keep.tile([P, PACK, H], F32, name="%s_raw" % name)
+            nc.sync.dma_start(raw[name][:], w.rearrange("(p j) c -> p j c", j=PACK))
         nc.sync.dma_start(w3_raw[:], w3.rearrange("(p j) m -> p j m", j=PACK))
 
         mag = keep.tile([P, PACK], F32, name="mag")
@@ -80,10 +73,9 @@ def tile_picked_yfairsp_cap_p_kernel(
         nc.vector.tensor_copy(x_plane[:], scales[:].indirect(offs_sb[:]))
 
         def deal(name, lo, hi, copy):
-            h = lo // (P // 2)
-            dst = grouped[name][:].rearrange("p t m j -> p m j t")[:, lo:hi, :, :]
-            src = raw[name, h][:].rearrange("p j (m t) -> p m j t", t=PACK)
-            copy(dst, src[:, lo - h * (P // 2) : hi - h * (P // 2), :, :])
+            dst = grouped[name][:].rearrange("p t m j -> p m j t")
+            src = raw[name][:].rearrange("p j (m t) -> p m j t", t=PACK)
+            copy(dst[:, lo:hi, :, :], src[:, lo:hi, :, :])
 
         def product(name, t):
             codes = keep.tile([P, P], U32, name="%s_codes%d" % (name, t), align_bytes=64)
@@ -99,18 +91,16 @@ def tile_picked_yfairsp_cap_p_kernel(
             return acc
 
         grouped = {}
-        for name in ("w1", "w2"):
-            grouped[name] = keep.tile([P, PACK, P, PACK], BF16, name="%s_grouped" % name, align_bytes=64)
-        deal("w1", 0, P // 2, nc.scalar.copy)
-        deal("w1", P // 2, SPLIT, nc.scalar.copy)
+        grouped["w1"] = keep.tile([P, PACK, P, PACK], BF16, name="w1_grouped", tag="grouped", align_bytes=64)
+        deal("w1", 0, SPLIT, nc.scalar.copy)
         deal("w1", SPLIT, P, nc.vector.tensor_copy)
         neg_y = []
         for t in range(PACK):
             y = product("w1", t)
             neg_y.append(keep.tile([P, WINDOW], F32, name="neg_y%d" % t))
             nc.scalar.activation(neg_y[t][:, :S], y[:], ACT.Copy, scale=neg[:, t : t + 1])
-        deal("w2", 0, P // 2, nc.vector.tensor_copy)
-        deal("w2", P // 2, P, nc.vector.tensor_copy)
+        grouped["w2"] = keep.tile([P, PACK, P, PACK], BF16, name="w2_grouped", tag="grouped", align_bytes=64)
+        deal("w2", 0, P, nc.vector.tensor_copy)
         z = [product("w2", t) for t in range(PACK)]
         score, signal = [], []
         for t in range(PACK):
@@ -123,17 +113,14 @@ def tile_picked_yfairsp_cap_p_kernel(
                 signal[t][:, :S], z[t][:], most[:, t : t + 1], neg_y[t][:, :S], ALU.mult, ALU.add
             )
 
-        w3_grouped = keep.tile([P, N, PACK], BF16, name="w3_grouped", align_bytes=64)
+        w3_grouped = keep.tile([P, N, PACK], BF16, name="w3_grouped", tag="grouped", align_bytes=64)
         w3_codes = keep.tile([P, N], U32, name="w3_codes", align_bytes=64)
         w3_plane = keep.tile([P, N], U8, name="w3_plane", align_bytes=64)
-        nc.vector.tensor_tensor(
+        nc.gpsimd.tensor_tensor(
             w3_grouped[:].rearrange("p (c i) j -> p c j i", i=2),
             w3_raw[:].rearrange("p j (c i) -> p c j i", i=2),
             sgn[:].unsqueeze(1).unsqueeze(3).to_broadcast([P, N // 2, PACK, 2]),
             ALU.mult,
-        )
-        nc.vector.quantize_mx(
-            out=w3_codes[:].bitcast(FP8X4), scales=w3_plane[:], in_=w3_grouped[:].rearrange("p m j -> p (m j)")
         )
 
         second_y = {}
@@ -148,11 +135,13 @@ def tile_picked_yfairsp_cap_p_kernel(
                 second_y[t] = keep.tile([P, hi - lo], F32, name="second_y%d" % t)
                 nc.scalar.activation(second_y[t][:], neg_y[t][:].indirect(entries(fb_sb, lo, hi)), ACT.Copy)
 
-        def fetch_signal(lo, hi):
+        def fetch_signal(lo, hi, on_vector=0):
             for t in range(PACK):
-                nc.scalar.activation(
-                    second_signal[:, t, lo:hi], signal[t][:].indirect(entries(fb_sb, lo, hi)), ACT.Copy
-                )
+                picked = signal[t][:].indirect(entries(fb_sb, lo, hi))
+                if t < PACK - on_vector:
+                    nc.scalar.activation(second_signal[:, t, lo:hi], picked, ACT.Copy)
+                else:
+                    nc.vector.tensor_copy(second_signal[:, t, lo:hi], picked)
 
         def fetch_score(lo, hi):
             lead[lo] = keep.tile([P, PACK, hi - lo], F32, name="lead")
@@ -193,15 +182,18 @@ def tile_picked_yfairsp_cap_p_kernel(
 
         fetch_y(0, 512)
         fetch_score(0, 512)
+        nc.vector.quantize_mx(
+            out=w3_codes[:].bitcast(FP8X4), scales=w3_plane[:], in_=w3_grouped[:].rearrange("p m j -> p (m j)")
+        )
         fetch_signal(0, 512)
         fetch_y(512, 1024)
         acc0 = finish(0, 256)
         acc1 = finish(256, 512)
         fetch_score(512, 1024)
         fetch_signal(512, 768)
-        fetch_signal(768, 1024)
-        store(0, 256, acc0, "signal2")
-        store(256, 512, acc1, "signal3")
+        fetch_signal(768, 1024, on_vector=1)
+        store(0, 256, acc0, "signal1")
+        store(256, 512, acc1, "signal2")
         store(512, 768, finish(512, 768), "result2")
         store(768, 896, finish(768, 896), "result3")
         store(896, 1024, finish(896, 1024), "result4")

@@ -191,9 +191,9 @@ def tile_picked_yfairsp_cap_p_kernel(
         acc1 = finish(256, 512)
         fetch_score(512, 1024)
         fetch_signal(512, 768)
-        fetch_signal(768, 1024, on_vector=1)
-        store(0, 256, acc0, "signal1")
-        store(256, 512, acc1, "signal2")
+        fetch_signal(768, 1024, on_vector=2)
+        store(0, 256, acc0, "signal0")
+        store(256, 512, acc1, "signal1")
         store(512, 768, finish(512, 768), "result2")
         store(768, 896, finish(768, 896), "result3")
         store(896, 1024, finish(896, 1024), "result4")

@@ -17,8 +17,14 @@ ACT = mybir.ActivationFunctionType
 
 P = 128
 PACK = 4
+QUADRANT = 32
+LIST_ROWS = 16
+BANKS = 8
+ROW_TILES = N // P
 WINDOW = S + 32
-SPLIT = 44
+HALF, QUARTER, EIGHTH = U // 2, U // 4, U // 8
+PIECES = 5
+PAIR = 2
 
 
 def tile_picked_yfairsp_cap_p_kernel(
@@ -27,11 +33,11 @@ def tile_picked_yfairsp_cap_p_kernel(
     nc = tc.nc
     with ExitStack() as ctx:
         keep = ctx.enter_context(tc.tile_pool(name="keep", bufs=1))
-        psum = ctx.enter_context(tc.psum_pool(name="psum", bufs=8))
+        psum = ctx.enter_context(tc.psum_pool(name="psum", bufs=BANKS))
 
-        offs_sb = keep.tile([P, S // 16], U16, name="offs_sb")
-        fa_sb = keep.tile([P, U // 16], U16, name="fa_sb")
-        fb_sb = keep.tile([P, U // 16], U16, name="fb_sb")
+        offs_sb = keep.tile([P, S // LIST_ROWS], U16, name="offs_sb")
+        fa_sb = keep.tile([P, U // LIST_ROWS], U16, name="fa_sb")
+        fb_sb = keep.tile([P, U // LIST_ROWS], U16, name="fb_sb")
         words = keep.tile([P, T], I32, name="words", align_bytes=64)
         scales = keep.tile([P, T], U8, name="scales", align_bytes=64)
         unit_sb = keep.tile([P, PACK], F32, name="unit_sb")
@@ -42,158 +48,173 @@ def tile_picked_yfairsp_cap_p_kernel(
         nc.sync.dma_start(offs_sb[:], offs)
         nc.sync.dma_start(unit_sb[:], unit.rearrange("(p t) o -> p (t o)", t=PACK))
         nc.sync.dma_start(words[:], x_words[0].rearrange("p c r -> p (c r)").bitcast(I32))
-        for q in range(4):
+        for q in range(P // QUADRANT):
             nc.sync.dma_start(
-                scales[32 * q : 32 * q + 4, :].bitcast(I32), x_scales[0, 4 * q : 4 * q + 4, :].bitcast(I32)
+                scales[QUADRANT * q : QUADRANT * q + 4, :].bitcast(I32),
+                x_scales[0, 4 * q : 4 * q + 4, :].bitcast(I32),
             )
         nc.sync.dma_start(fb_sb[:], fb)
-        nc.sync.dma_start(fa_sb[:], fa)
         raw = {}
         for name, w in (("w1", w1), ("w2", w2)):
             raw[name] = keep.tile([P, PACK, H], F32, name="%s_raw" % name)
             nc.sync.dma_start(raw[name][:], w.rearrange("(p j) c -> p j c", j=PACK))
+        nc.sync.dma_start(fa_sb[:], fa)
         nc.sync.dma_start(w3_raw[:], w3.rearrange("(p j) m -> p j m", j=PACK))
 
         mag = keep.tile([P, PACK], F32, name="mag")
-        neg = keep.tile([P, PACK], F32, name="neg")
-        half = keep.tile([P, PACK], F32, name="half")
-        most = keep.tile([P, PACK], F32, name="most")
+        neg_mag = keep.tile([P, PACK], F32, name="neg_mag")
+        score_mag = keep.tile([P, PACK], F32, name="score_mag")
+        signal_mag = keep.tile([P, PACK], F32, name="signal_mag")
         step = keep.tile([P, PACK], F32, name="step")
         sgn = keep.tile([P, PACK], F32, name="sgn")
         nc.scalar.activation(mag[:], unit_sb[:], ACT.Abs)
-        nc.scalar.activation(neg[:], mag[:], ACT.Copy, scale=-1.0)
-        nc.scalar.activation(half[:], mag[:], ACT.Copy, scale=0.5)
-        nc.scalar.activation(most[:], mag[:], ACT.Copy, scale=0.8)
+        nc.scalar.activation(neg_mag[:], mag[:], ACT.Copy, scale=-1.0)
+        nc.scalar.activation(score_mag[:], mag[:], ACT.Copy, scale=0.5)
+        nc.scalar.activation(signal_mag[:], mag[:], ACT.Copy, scale=0.8)
         nc.vector.tensor_scalar(step[:], unit_sb[:], 0.0, 2.0, ALU.is_ge, ALU.mult)
         nc.vector.tensor_scalar(sgn[:], step[:], -1.0, None, ALU.add)
 
         x_codes = keep.tile([P, S], U32, name="x_codes", align_bytes=64)
-        x_plane = keep.tile([P, S], U8, name="x_plane", align_bytes=64)
+        x_bytes = keep.tile([P, S], U8, name="x_bytes", align_bytes=64)
         nc.vector.tensor_copy(x_codes[:], words[:].bitcast(U32).indirect(offs_sb[:]))
-        nc.vector.tensor_copy(x_plane[:], scales[:].indirect(offs_sb[:]))
+        nc.vector.tensor_copy(x_bytes[:], scales[:].indirect(offs_sb[:]))
 
-        def deal(name, lo, hi, copy):
-            dst = grouped[name][:].rearrange("p t m j -> p m j t")
+        staged = {}
+
+        def deal(name, t0, copy):
+            dst = staged[name][:].rearrange("p t m j -> p m j t")
             src = raw[name][:].rearrange("p j (m t) -> p m j t", t=PACK)
-            copy(dst[:, lo:hi, :, :], src[:, lo:hi, :, :])
+            copy(dst[:, :, :, t0 : t0 + 2], src[:, :, :, t0 : t0 + 2])
 
         def product(name, t):
             codes = keep.tile([P, P], U32, name="%s_codes%d" % (name, t), align_bytes=64)
-            plane = keep.tile([P, P], U8, name="%s_plane%d" % (name, t), align_bytes=64)
+            scale_bytes = keep.tile([P, P], U8, name="%s_bytes%d" % (name, t), align_bytes=64)
             nc.vector.quantize_mx(
-                out=codes[:].bitcast(FP8X4), scales=plane[:], in_=grouped[name][:, t].rearrange("p m j -> p (m j)")
+                out=codes[:].bitcast(FP8X4),
+                scales=scale_bytes[:],
+                in_=staged[name][:, t].rearrange("p m j -> p (m j)"),
             )
             acc = psum.tile([P, S], F32, name="acc")
             nc.tensor.matmul_mx(
-                out=acc[:], lhsT=codes[:].bitcast(FP8X4), lhsT_scale=plane[:],
-                rhs=x_codes[:].bitcast(FP8X4), rhs_scale=x_plane[:], start=True, stop=True,
+                out=acc[:], lhsT=codes[:].bitcast(FP8X4), lhsT_scale=scale_bytes[:],
+                rhs=x_codes[:].bitcast(FP8X4), rhs_scale=x_bytes[:], start=True, stop=True,
             )
             return acc
 
-        grouped = {}
-        grouped["w1"] = keep.tile([P, PACK, P, PACK], BF16, name="w1_grouped", tag="grouped", align_bytes=64)
-        deal("w1", 0, SPLIT, nc.scalar.copy)
-        deal("w1", SPLIT, P, nc.vector.tensor_copy)
+        staged["w1"] = keep.tile([P, PACK, P, PACK], BF16, name="w1_staged", tag="staged", align_bytes=64)
+        deal("w1", 0, nc.vector.tensor_copy)
+        deal("w1", 2, nc.scalar.copy)
         neg_y = []
         for t in range(PACK):
             y = product("w1", t)
-            neg_y.append(keep.tile([P, WINDOW], F32, name="neg_y%d" % t))
-            nc.scalar.activation(neg_y[t][:, :S], y[:], ACT.Copy, scale=neg[:, t : t + 1])
-        grouped["w2"] = keep.tile([P, PACK, P, PACK], BF16, name="w2_grouped", tag="grouped", align_bytes=64)
-        deal("w2", 0, P, nc.vector.tensor_copy)
-        z = [product("w2", t) for t in range(PACK)]
+            neg_y.append(keep.tile([P, WINDOW], F32, name="neg_y%d" % t, tag="neg_y%d" % t))
+            nc.scalar.activation(neg_y[t][:, :S], y[:], ACT.Copy, scale=neg_mag[:, t : t + 1])
+        staged["w2"] = keep.tile([P, PACK, P, PACK], BF16, name="w2_staged", tag="staged", align_bytes=64)
+        z1 = []
+        for t0 in (0, 2):
+            deal("w2", t0, nc.vector.tensor_copy)
+            z1.extend([product("w2", t0), product("w2", t0 + 1)])
         score, signal = [], []
         for t in range(PACK):
             score.append(keep.tile([P, WINDOW], F32, name="score%d" % t))
             signal.append(keep.tile([P, WINDOW], F32, name="signal%d" % t, tag="signal%d" % t))
             nc.vector.scalar_tensor_tensor(
-                score[t][:, :S], z[t][:], half[:, t : t + 1], neg_y[t][:, :S], ALU.mult, ALU.subtract
+                score[t][:, :S], z1[t][:], score_mag[:, t : t + 1], neg_y[t][:, :S], ALU.mult, ALU.subtract
             )
             nc.vector.scalar_tensor_tensor(
-                signal[t][:, :S], z[t][:], most[:, t : t + 1], neg_y[t][:, :S], ALU.mult, ALU.add
+                signal[t][:, :S], z1[t][:], signal_mag[:, t : t + 1], neg_y[t][:, :S], ALU.mult, ALU.add
             )
 
-        w3_grouped = keep.tile([P, N, PACK], BF16, name="w3_grouped", tag="grouped", align_bytes=64)
+        w3_staged = keep.tile([P, N, PACK], BF16, name="w3_staged", tag="staged", align_bytes=64)
         w3_codes = keep.tile([P, N], U32, name="w3_codes", align_bytes=64)
-        w3_plane = keep.tile([P, N], U8, name="w3_plane", align_bytes=64)
+        w3_bytes = keep.tile([P, N], U8, name="w3_bytes", align_bytes=64)
         nc.gpsimd.tensor_tensor(
-            w3_grouped[:].rearrange("p (c i) j -> p c j i", i=2),
-            w3_raw[:].rearrange("p j (c i) -> p c j i", i=2),
-            sgn[:].unsqueeze(1).unsqueeze(3).to_broadcast([P, N // 2, PACK, 2]),
+            w3_staged[:].rearrange("p (c i) j -> p c j i", i=PAIR),
+            w3_raw[:].rearrange("p j (c i) -> p c j i", i=PAIR),
+            sgn[:].unsqueeze(1).unsqueeze(3).to_broadcast([P, N // PAIR, PACK, PAIR]),
             ALU.mult,
         )
 
-        second_y = {}
-        second_signal = keep.tile([P, PACK, U], F32, name="second_signal")
-        lead = {}
+        def entries(list_sb, lo, hi):
+            return list_sb[:, lo // LIST_ROWS : hi // LIST_ROWS]
 
-        def entries(lst, lo, hi):
-            return lst[:, lo // 16 : hi // 16]
-
-        def fetch_y(lo, hi):
+        def fetch_y(lo):
+            picked = []
             for t in range(PACK):
-                second_y[t] = keep.tile([P, hi - lo], F32, name="second_y%d" % t)
-                nc.scalar.activation(second_y[t][:], neg_y[t][:].indirect(entries(fb_sb, lo, hi)), ACT.Copy)
+                picked.append(keep.tile([P, HALF], F32, name="picked_y%d" % t))
+                nc.scalar.activation(picked[t][:], neg_y[t][:].indirect(entries(fb_sb, lo, lo + HALF)), ACT.Copy)
+            return picked
 
-        def fetch_signal(lo, hi, on_vector=0):
-            for t in range(PACK):
-                picked = signal[t][:].indirect(entries(fb_sb, lo, hi))
-                if t < PACK - on_vector:
-                    nc.scalar.activation(second_signal[:, t, lo:hi], picked, ACT.Copy)
-                else:
-                    nc.vector.tensor_copy(second_signal[:, t, lo:hi], picked)
-
-        def fetch_score(lo, hi):
-            lead[lo] = keep.tile([P, PACK, hi - lo], F32, name="lead")
+        def fetch_lead(lo, picked_y):
+            lead = keep.tile([P, PACK, HALF], F32, name="lead")
             for t in range(PACK):
                 nc.vector.tensor_tensor(
-                    lead[lo][:, t, :], score[t][:].indirect(entries(fa_sb, lo, hi)), second_y[t][:], ALU.add
+                    lead[:, t, :], score[t][:].indirect(entries(fa_sb, lo, lo + HALF)), picked_y[t][:], ALU.add
                 )
+            return lead
 
-        def finish(lo, hi):
-            n = hi - lo
-            base = lo // 512 * 512
-            hid = keep.tile([P, n, PACK], BF16, name="hid%d" % lo, align_bytes=64)
-            codes = keep.tile([P, n], U32, name="hid_codes%d" % lo, align_bytes=64)
-            plane = keep.tile([P, n], U8, name="hid_plane%d" % lo, align_bytes=64)
+        def fetch_signal(lo, hi, planes, tag):
+            picked = keep.tile([P, PACK, hi - lo], F32, name="picked_signal%d" % lo, tag=tag)
+            for t in planes:
+                nc.scalar.activation(picked[:, t, :], signal[t][:].indirect(entries(fb_sb, lo, hi)), ACT.Copy)
+            return picked
+
+        def finish(lead, picked_signal, tag):
+            n = lead.shape[2]
+            hid = keep.tile([P, n, PACK], BF16, name="hid", tag=tag, align_bytes=64)
+            codes = keep.tile([P, n], U32, name="hid_codes", bufs=PIECES, align_bytes=64)
+            scale_bytes = keep.tile([P, n], U8, name="hid_bytes", bufs=PIECES, align_bytes=64)
             nc.vector.tensor_tensor(
-                hid[:].rearrange("p (c i) t -> p c t i", i=2),
-                lead[base][:, :, lo - base : hi - base].rearrange("p t (c i) -> p c t i", i=2),
-                second_signal[:, :, lo:hi].rearrange("p t (c i) -> p c t i", i=2),
+                hid[:].rearrange("p (c i) t -> p c t i", i=PAIR),
+                lead.rearrange("p t (c i) -> p c t i", i=PAIR),
+                picked_signal.rearrange("p t (c i) -> p c t i", i=PAIR),
                 ALU.max,
             )
             nc.vector.quantize_mx(
-                out=codes[:].bitcast(FP8X4), scales=plane[:], in_=hid[:].rearrange("p r t -> p (r t)")
+                out=codes[:].bitcast(FP8X4), scales=scale_bytes[:], in_=hid[:].rearrange("p r t -> p (r t)")
             )
-            acc = psum.tile([P, 2, n], F32, name="acc")
-            for mt in range(2):
+            acc = psum.tile([P, ROW_TILES, n], F32, name="acc")
+            for mt in range(ROW_TILES):
                 nc.tensor.matmul_mx(
                     out=acc[:, mt, :],
                     lhsT=w3_codes[:, mt * P : (mt + 1) * P].bitcast(FP8X4),
-                    lhsT_scale=w3_plane[:, mt * P : (mt + 1) * P],
-                    rhs=codes[:].bitcast(FP8X4), rhs_scale=plane[:], start=True, stop=True,
+                    lhsT_scale=w3_bytes[:, mt * P : (mt + 1) * P],
+                    rhs=codes[:].bitcast(FP8X4), rhs_scale=scale_bytes[:], start=True, stop=True,
                 )
             return acc
 
-        def store(lo, hi, acc, tag):
-            result = keep.tile([P, 2, hi - lo], F32, name="result%d" % lo, tag=tag)
-            nc.scalar.copy(result[:], acc[:])
-            nc.sync.dma_start(out.rearrange("(mt p) r -> p mt r", p=P)[:, :, lo:hi], result[:])
+        def store(lo, acc, result, copy):
+            copy(result, acc[:])
+            nc.sync.dma_start(out.rearrange("(mt p) r -> p mt r", p=P)[:, :, lo : lo + acc.shape[2]], result)
 
-        fetch_y(0, 512)
-        fetch_score(0, 512)
+        picked_y = fetch_y(0)
+        lead = fetch_lead(0, picked_y)
         nc.vector.quantize_mx(
-            out=w3_codes[:].bitcast(FP8X4), scales=w3_plane[:], in_=w3_grouped[:].rearrange("p m j -> p (m j)")
+            out=w3_codes[:].bitcast(FP8X4), scales=w3_bytes[:], in_=w3_staged[:].rearrange("p m j -> p (m j)")
         )
-        fetch_signal(0, 512)
-        fetch_y(512, 1024)
-        acc0 = finish(0, 256)
-        acc1 = finish(256, 512)
-        fetch_score(512, 1024)
-        fetch_signal(512, 768)
-        fetch_signal(768, 1024, on_vector=2)
-        store(0, 256, acc0, "signal0")
-        store(256, 512, acc1, "signal1")
-        store(512, 768, finish(512, 768), "result2")
-        store(768, 896, finish(768, 896), "result3")
-        store(896, 1024, finish(896, 1024), "result4")
+        picked_signal = fetch_signal(0, HALF, range(PACK), "picked_signal")
+        picked_y = fetch_y(HALF)
+        first = finish(lead[:, :, :QUARTER], picked_signal[:, :, :QUARTER], "hid_even")
+        second = finish(lead[:, :, QUARTER:], picked_signal[:, :, QUARTER:], "hid_odd")
+
+        lead = fetch_lead(HALF, picked_y)
+        last = HALF + QUARTER
+        third_signal = fetch_signal(HALF, last, range(PACK), "neg_y%d" % (PACK - 1))
+        last_signal = fetch_signal(last, U, range(PACK - 1), "picked_signal")
+        nc.vector.tensor_copy(
+            last_signal[:, PACK - 1, :EIGHTH], signal[PACK - 1][:].indirect(entries(fb_sb, last, last + EIGHTH))
+        )
+        early = keep.tile([P, 2, ROW_TILES, QUARTER], F32, name="early", tag="signal%d" % (PACK - 2))
+        late = [
+            keep.tile([P, ROW_TILES, n], F32, name="late%d" % i) for i, n in enumerate((QUARTER, EIGHTH, EIGHTH))
+        ]
+        store(0, first, early[:, 0], nc.scalar.copy)
+        store(QUARTER, second, early[:, 1], nc.scalar.copy)
+        store(HALF, finish(lead[:, :, :QUARTER], third_signal[:], "hid_even"), late[0][:], nc.scalar.copy)
+        acc = finish(lead[:, :, QUARTER : QUARTER + EIGHTH], last_signal[:, :, :EIGHTH], "hid_odd")
+        store(last, acc, late[1][:], nc.scalar.copy)
+        nc.vector.tensor_copy(
+            last_signal[:, PACK - 1, EIGHTH:], signal[PACK - 1][:].indirect(entries(fb_sb, last + EIGHTH, U))
+        )
+        acc = finish(lead[:, :, QUARTER + EIGHTH :], last_signal[:, :, EIGHTH:], "hid_odd")
+        store(last + EIGHTH, acc, late[2][:], nc.vector.tensor_copy)

from contextlib import ExitStack

import concourse.mybir as mybir

K, T, S, N, H, U = 512, 2048, 512, 256, 512, 1024
FLOPS = 2 * (2 * K * H * S + H * N * U)

F32 = mybir.dt.float32
BF16 = mybir.dt.bfloat16
I32 = mybir.dt.int32
U32 = mybir.dt.uint32
U16 = mybir.dt.uint16
U8 = mybir.dt.uint8
FP8X4 = mybir.dt.float8_e4m3fn_x4
ALU = mybir.AluOpType
ACT = mybir.ActivationFunctionType

P = 128
PACK = 4
QUADRANT = 32
LIST_ROWS = 16
BANKS = 8
ROW_TILES = N // P
WINDOW = S + 32
HALF, QUARTER, EIGHTH = U // 2, U // 4, U // 8
PIECES = 5
PAIR = 2


def tile_picked_yfairsp_cap_p_kernel(
    tc, x_words, x_scales, w1, w2, unit, w3, offs, fa, fb, out
):
    nc = tc.nc
    with ExitStack() as ctx:
        keep = ctx.enter_context(tc.tile_pool(name="keep", bufs=1))
        psum = ctx.enter_context(tc.psum_pool(name="psum", bufs=BANKS))

        offs_sb = keep.tile([P, S // LIST_ROWS], U16, name="offs_sb")
        fa_sb = keep.tile([P, U // LIST_ROWS], U16, name="fa_sb")
        fb_sb = keep.tile([P, U // LIST_ROWS], U16, name="fb_sb")
        words = keep.tile([P, T], I32, name="words", align_bytes=64)
        scales = keep.tile([P, T], U8, name="scales", align_bytes=64)
        unit_sb = keep.tile([P, PACK], F32, name="unit_sb")
        w3_raw = keep.tile([P, PACK, N], F32, name="w3_raw")

        nc.vector.memset(scales[:, : T // 2].bitcast(I32), 0)
        nc.gpsimd.memset(scales[:, T // 2 :].bitcast(I32), 0)
        nc.sync.dma_start(offs_sb[:], offs)
        nc.sync.dma_start(unit_sb[:], unit.rearrange("(p t) o -> p (t o)", t=PACK))
        nc.sync.dma_start(words[:], x_words[0].rearrange("p c r -> p (c r)").bitcast(I32))
        for q in range(P // QUADRANT):
            nc.sync.dma_start(
                scales[QUADRANT * q : QUADRANT * q + 4, :].bitcast(I32),
                x_scales[0, 4 * q : 4 * q + 4, :].bitcast(I32),
            )
        nc.sync.dma_start(fb_sb[:], fb)
        raw = {}
        for name, w in (("w1", w1), ("w2", w2)):
            raw[name] = keep.tile([P, PACK, H], F32, name="%s_raw" % name)
            nc.sync.dma_start(raw[name][:], w.rearrange("(p j) c -> p j c", j=PACK))
        nc.sync.dma_start(fa_sb[:], fa)
        nc.sync.dma_start(w3_raw[:], w3.rearrange("(p j) m -> p j m", j=PACK))

        mag = keep.tile([P, PACK], F32, name="mag")
        neg_mag = keep.tile([P, PACK], F32, name="neg_mag")
        score_mag = keep.tile([P, PACK], F32, name="score_mag")
        signal_mag = keep.tile([P, PACK], F32, name="signal_mag")
        step = keep.tile([P, PACK], F32, name="step")
        sgn = keep.tile([P, PACK], F32, name="sgn")
        nc.scalar.activation(mag[:], unit_sb[:], ACT.Abs)
        nc.scalar.activation(neg_mag[:], mag[:], ACT.Copy, scale=-1.0)
        nc.scalar.activation(score_mag[:], mag[:], ACT.Copy, scale=0.5)
        nc.scalar.activation(signal_mag[:], mag[:], ACT.Copy, scale=0.8)
        nc.vector.tensor_scalar(step[:], unit_sb[:], 0.0, 2.0, ALU.is_ge, ALU.mult)
        nc.vector.tensor_scalar(sgn[:], step[:], -1.0, None, ALU.add)

        x_codes = keep.tile([P, S], U32, name="x_codes", align_bytes=64)
        x_bytes = keep.tile([P, S], U8, name="x_bytes", align_bytes=64)
        nc.vector.tensor_copy(x_codes[:], words[:].bitcast(U32).indirect(offs_sb[:]))
        nc.vector.tensor_copy(x_bytes[:], scales[:].indirect(offs_sb[:]))

        staged = {}

        def deal(name, t0, copy):
            dst = staged[name][:].rearrange("p t m j -> p m j t")
            src = raw[name][:].rearrange("p j (m t) -> p m j t", t=PACK)
            copy(dst[:, :, :, t0 : t0 + 2], src[:, :, :, t0 : t0 + 2])

        def product(name, t):
            codes = keep.tile([P, P], U32, name="%s_codes%d" % (name, t), align_bytes=64)
            scale_bytes = keep.tile([P, P], U8, name="%s_bytes%d" % (name, t), align_bytes=64)
            nc.vector.quantize_mx(
                out=codes[:].bitcast(FP8X4),
                scales=scale_bytes[:],
                in_=staged[name][:, t].rearrange("p m j -> p (m j)"),
            )
            acc = psum.tile([P, S], F32, name="acc")
            nc.tensor.matmul_mx(
                out=acc[:], lhsT=codes[:].bitcast(FP8X4), lhsT_scale=scale_bytes[:],
                rhs=x_codes[:].bitcast(FP8X4), rhs_scale=x_bytes[:], start=True, stop=True,
            )
            return acc

        staged["w1"] = keep.tile([P, PACK, P, PACK], BF16, name="w1_staged", tag="staged", align_bytes=64)
        deal("w1", 0, nc.vector.tensor_copy)
        deal("w1", 2, nc.scalar.copy)
        neg_y = []
        for t in range(PACK):
            y = product("w1", t)
            neg_y.append(keep.tile([P, WINDOW], F32, name="neg_y%d" % t, tag="neg_y%d" % t))
            nc.scalar.activation(neg_y[t][:, :S], y[:], ACT.Copy, scale=neg_mag[:, t : t + 1])
        staged["w2"] = keep.tile([P, PACK, P, PACK], BF16, name="w2_staged", tag="staged", align_bytes=64)
        z1 = []
        for t0 in (0, 2):
            deal("w2", t0, nc.vector.tensor_copy)
            z1.extend([product("w2", t0), product("w2", t0 + 1)])
        score, signal = [], []
        for t in range(PACK):
            score.append(keep.tile([P, WINDOW], F32, name="score%d" % t))
            signal.append(keep.tile([P, WINDOW], F32, name="signal%d" % t, tag="signal%d" % t))
            nc.vector.scalar_tensor_tensor(
                score[t][:, :S], z1[t][:], score_mag[:, t : t + 1], neg_y[t][:, :S], ALU.mult, ALU.subtract
            )
            nc.vector.scalar_tensor_tensor(
                signal[t][:, :S], z1[t][:], signal_mag[:, t : t + 1], neg_y[t][:, :S], ALU.mult, ALU.add
            )

        w3_staged = keep.tile([P, N, PACK], BF16, name="w3_staged", tag="staged", align_bytes=64)
        w3_codes = keep.tile([P, N], U32, name="w3_codes", align_bytes=64)
        w3_bytes = keep.tile([P, N], U8, name="w3_bytes", align_bytes=64)
        nc.gpsimd.tensor_tensor(
            w3_staged[:].rearrange("p (c i) j -> p c j i", i=PAIR),
            w3_raw[:].rearrange("p j (c i) -> p c j i", i=PAIR),
            sgn[:].unsqueeze(1).unsqueeze(3).to_broadcast([P, N // PAIR, PACK, PAIR]),
            ALU.mult,
        )

        def entries(list_sb, lo, hi):
            return list_sb[:, lo // LIST_ROWS : hi // LIST_ROWS]

        def fetch_y(lo):
            picked = []
            for t in range(PACK):
                picked.append(keep.tile([P, HALF], F32, name="picked_y%d" % t))
                nc.scalar.activation(picked[t][:], neg_y[t][:].indirect(entries(fb_sb, lo, lo + HALF)), ACT.Copy)
            return picked

        def fetch_lead(lo, picked_y):
            lead = keep.tile([P, PACK, HALF], F32, name="lead")
            for t in range(PACK):
                nc.vector.tensor_tensor(
                    lead[:, t, :], score[t][:].indirect(entries(fa_sb, lo, lo + HALF)), picked_y[t][:], ALU.add
                )
            return lead

        def fetch_signal(lo, hi, planes, tag):
            picked = keep.tile([P, PACK, hi - lo], F32, name="picked_signal%d" % lo, tag=tag)
            for t in planes:
                nc.scalar.activation(picked[:, t, :], signal[t][:].indirect(entries(fb_sb, lo, hi)), ACT.Copy)
            return picked

        def finish(lead, picked_signal, tag):
            n = lead.shape[2]
            hid = keep.tile([P, n, PACK], BF16, name="hid", tag=tag, align_bytes=64)
            codes = keep.tile([P, n], U32, name="hid_codes", bufs=PIECES, align_bytes=64)
            scale_bytes = keep.tile([P, n], U8, name="hid_bytes", bufs=PIECES, align_bytes=64)
            nc.vector.tensor_tensor(
                hid[:].rearrange("p (c i) t -> p c t i", i=PAIR),
                lead.rearrange("p t (c i) -> p c t i", i=PAIR),
                picked_signal.rearrange("p t (c i) -> p c t i", i=PAIR),
                ALU.max,
            )
            nc.vector.quantize_mx(
                out=codes[:].bitcast(FP8X4), scales=scale_bytes[:], in_=hid[:].rearrange("p r t -> p (r t)")
            )
            acc = psum.tile([P, ROW_TILES, n], F32, name="acc")
            for mt in range(ROW_TILES):
                nc.tensor.matmul_mx(
                    out=acc[:, mt, :],
                    lhsT=w3_codes[:, mt * P : (mt + 1) * P].bitcast(FP8X4),
                    lhsT_scale=w3_bytes[:, mt * P : (mt + 1) * P],
                    rhs=codes[:].bitcast(FP8X4), rhs_scale=scale_bytes[:], start=True, stop=True,
                )
            return acc

        def store(lo, acc, result, copy):
            copy(result, acc[:])
            nc.sync.dma_start(out.rearrange("(mt p) r -> p mt r", p=P)[:, :, lo : lo + acc.shape[2]], result)

        picked_y = fetch_y(0)
        lead = fetch_lead(0, picked_y)
        nc.vector.quantize_mx(
            out=w3_codes[:].bitcast(FP8X4), scales=w3_bytes[:], in_=w3_staged[:].rearrange("p m j -> p (m j)")
        )
        picked_signal = fetch_signal(0, HALF, range(PACK), "picked_signal")
        picked_y = fetch_y(HALF)
        first = finish(lead[:, :, :QUARTER], picked_signal[:, :, :QUARTER], "hid_even")
        second = finish(lead[:, :, QUARTER:], picked_signal[:, :, QUARTER:], "hid_odd")

        lead = fetch_lead(HALF, picked_y)
        last = HALF + QUARTER
        third_signal = fetch_signal(HALF, last, range(PACK), "neg_y%d" % (PACK - 1))
        last_signal = fetch_signal(last, U, range(PACK - 1), "picked_signal")
        nc.vector.tensor_copy(
            last_signal[:, PACK - 1, :EIGHTH], signal[PACK - 1][:].indirect(entries(fb_sb, last, last + EIGHTH))
        )
        early = keep.tile([P, 2, ROW_TILES, QUARTER], F32, name="early", tag="signal%d" % (PACK - 2))
        late = [
            keep.tile([P, ROW_TILES, n], F32, name="late%d" % i) for i, n in enumerate((QUARTER, EIGHTH, EIGHTH))
        ]
        store(0, first, early[:, 0], nc.scalar.copy)
        store(QUARTER, second, early[:, 1], nc.scalar.copy)
        store(HALF, finish(lead[:, :, :QUARTER], third_signal[:], "hid_even"), late[0][:], nc.scalar.copy)
        acc = finish(lead[:, :, QUARTER : QUARTER + EIGHTH], last_signal[:, :, :EIGHTH], "hid_odd")
        store(last, acc, late[1][:], nc.scalar.copy)
        nc.vector.tensor_copy(
            last_signal[:, PACK - 1, EIGHTH:], signal[PACK - 1][:].indirect(entries(fb_sb, last + EIGHTH, U))
        )
        acc = finish(lead[:, :, QUARTER + EIGHTH :], last_signal[:, :, EIGHTH:], "hid_odd")
        store(last + EIGHTH, acc, late[2][:], nc.vector.tensor_copy)
